import numpy as np
import ml_dtypes


def mxq(x, axis, fmt="e4m3"):
    dtype, down = {"e4m3": (ml_dtypes.float8_e4m3fn, 7), "e5m2": (ml_dtypes.float8_e5m2, 14)}[fmt]
    v = np.moveaxis(np.asarray(x, np.float32).astype(ml_dtypes.bfloat16).astype(np.float64), axis, -1)
    blocks = v.reshape(v.shape[:-1] + (-1, 32))
    amax = np.abs(blocks).max(-1, keepdims=True)
    byte = np.maximum(np.where(amax > 0, np.frexp(amax)[1] - 1 + 127, 0) - down, 1)
    scale = np.exp2(byte - 127.0)
    codes = (blocks / scale).astype(np.float32).astype(dtype).astype(np.float64)
    return np.moveaxis((codes * scale).reshape(v.shape), -1, axis)


WIDE = False


def mx_kscale(k):
    if not WIDE:
        return np.ones(k)
    levels = np.array([10, -10, 5, -5, 0])
    if k % 512:
        return np.exp2(np.random.permutation(np.resize(levels, k // 32))).repeat(32)
    a = np.empty((k // 512, 16))
    for p in range(k // 512):
        a[p, :8] = np.random.permutation(np.resize(levels, 8))
        for g in range(8):
            far = levels[np.abs(levels - a[p, g]) >= 10]
            a[p, g + 8] = far[np.random.randint(len(far))]
    return np.exp2(a.ravel()).repeat(32)


def f64(x):
    return np.asarray(x).astype(np.float64)


def striped(idx):
    return np.tile(idx.reshape(-1, 16).T, (8, 1)).astype(np.uint16)


def unstriped(offs):
    return offs[:16].T.reshape(-1).astype(np.int64)


E2M1 = np.array([0.0, 0.5, 1.0, 1.5, 2.0, 3.0, 4.0, 6.0, -0.0, -0.5, -1.0, -1.5, -2.0, -3.0, -4.0, -6.0])


def pack_weight(w, fmt):
    k, n = w.shape
    w = f64(np.asarray(w, np.float32).astype(ml_dtypes.bfloat16)).reshape(k // 32, 32, n)
    amax = np.abs(w).max(1)
    if fmt == "e4m3":
        byte = np.frexp(amax)[1] - 1 + 127 - 7
    else:
        mant, ex = np.frexp(amax / 6.0)
        byte = np.where(mant > 0.5, ex, ex - 1) + 127
    byte = np.clip(np.where(amax > 0, byte, 1), 1, 254)
    scaled = (w * np.exp2(127.0 - byte)[:, None, :]).reshape(k, n).astype(np.float32)
    by_word = np.ascontiguousarray(scaled.reshape(k // 512, 128, 4, n).transpose(0, 1, 3, 2))
    if fmt == "e4m3":
        words = by_word.astype(ml_dtypes.float8_e4m3fn).view(np.uint8)
    else:
        c = by_word.astype(ml_dtypes.float4_e2m1fn).view(np.uint8) & 0xF
        words = (c[..., 0::2] | (c[..., 1::2] << 4)).reshape(k // 512, 128, 2 * n)
    return np.ascontiguousarray(words), np.ascontiguousarray(byte.astype(np.uint8).reshape(k // 512, 16, n))


def unpack_weight(words, scales, fmt):
    g, _, n = scales.shape
    words = np.ascontiguousarray(words).reshape(g, 128, n, -1)
    if fmt == "e4m3":
        vals = words.view(ml_dtypes.float8_e4m3fn).astype(np.float64)
    else:
        nib = np.empty((g, 128, n, 4), np.uint8)
        nib[..., 0::2] = words & 0xF
        nib[..., 1::2] = words >> 4
        vals = E2M1[nib]
    vals = vals * np.repeat(np.exp2(scales.astype(np.float64) - 127.0), 8, axis=1)[..., None]
    return vals.transpose(0, 1, 3, 2).reshape(g * 512, n)


def gelu(v):
    return 0.5 * v * (1.0 + np.tanh(np.sqrt(2.0 / np.pi) * (v + 0.044715 * v**3)))


K, H, T, S, T3, S2, P = 1024, 1024, 4096, 1024, 2048, 512, 512

def setup_inputs():
    n = np.random.standard_normal
    s = mx_kscale(K)[:, None]
    u = mx_kscale(H)[:, None]
    tab_words, tab_scales = pack_weight(n((K, T)) * s, "e4m3")
    tab2_words, tab2_scales = pack_weight(n((H, T3)) / np.sqrt(H) / u, "e4m3")
    w1 = (np.eye(K, H) + n((K, H)) / np.sqrt(K)) / s
    w4_words, w4_scales = pack_weight(n((K, H)) / np.sqrt(K) / s, "e2m1")
    return {
        "tab_words": tab_words, "tab_scales": tab_scales,
        "tab2_words": tab2_words, "tab2_scales": tab2_scales,
        "w1": w1.astype(np.float32),
        "w4_words": w4_words, "w4_scales": w4_scales,
        "gain": (np.exp(0.3 * n(H)) * u[:, 0]).astype(np.float32),
        "opening": (n(H) * u[:, 0]).astype(np.float32),
        "cue": np.random.uniform(0.25, 1.25, (S2, P)).astype(np.float32),
        "offs": striped(np.random.permutation(T)[:S]),
        "offs2": striped(np.random.permutation(T3)[:S2]),
        "pos1": striped(np.random.permutation(S)[:P]),
        "pos2": striped(np.random.permutation(S)[:P]),
    }

def reference(tab_words, tab_scales, tab2_words, tab2_scales, w1, w4_words, w4_scales, gain, opening, cue, offs, offs2, pos1, pos2):
    v = unpack_weight(tab_words, tab_scales, "e4m3")[:, unstriped(offs)]
    v2 = unpack_weight(tab2_words, tab2_scales, "e4m3")[:, unstriped(offs2)]
    w4 = unpack_weight(w4_words, w4_scales, "e2m1")
    own = mxq(f64(w1), 0, "e4m3").T @ v
    other = w4.T @ v
    h = np.maximum(own, other) * f64(gain)[:, None]
    x1 = mxq(h[:, unstriped(pos1)] + f64(opening)[:, None], 0, "e4m3")
    x2 = mxq(h[:, unstriped(pos2)], 0, "e4m3")
    e1 = v2.T @ x1
    e2 = v2.T @ x2
    return e1 * e2 * f64(cue)

@@ -1,0 +1,313 @@
+from contextlib import ExitStack
+
+import concourse.mybir as mybir
+
+K, H, T, S, T3, S2, P2 = 1024, 1024, 4096, 1024, 2048, 512, 512
+FLOPS = 2 * 2 * K * H * S + 2 * 2 * H * S2 * P2
+
+F32 = mybir.dt.float32
+BF16 = mybir.dt.bfloat16
+I32 = mybir.dt.int32
+U32 = mybir.dt.uint32
+U16 = mybir.dt.uint16
+U8 = mybir.dt.uint8
+FP8X4 = mybir.dt.float8_e4m3fn_x4
+FP4X4 = mybir.dt.float4_e2m1fn_x4
+ALU = mybir.AluOpType
+IDENT = mybir.ActivationFunctionType.Identity
+
+P = 128
+PACK = 4
+PASS = P * PACK
+BANK = 512
+
+
+def tile_list_runway_look_order_kernel(
+    tc, tab_words, tab_scales, tab2_words, tab2_scales, w1, w4_words, w4_scales,
+    gain, opening, cue, offs, offs2, pos1, pos2, out,
+):
+    nc = tc.nc
+    with ExitStack() as ctx:
+        keep = ctx.enter_context(tc.tile_pool(name="keep", bufs=1))
+        ring = ctx.enter_context(tc.tile_pool(name="ring", bufs=4))
+        psum = ctx.enter_context(tc.psum_pool(name="psum", bufs=1))
+
+        def held(shape, dtype, name):
+            return keep.tile(shape, dtype, name=name, align_bytes=64)
+
+        offs_t = held([P, S // 16], U16, "offs_t")
+        offs2_t = held([P, S2 // 16], U16, "offs2_t")
+        pos_t = [held([P, P2 // 16], U16, "pos%d_t" % i) for i in range(2)]
+        tab_w = [held([P, T], I32, "tab_w%d" % a) for a in range(2)]
+        tab_s = held([P, 2, T], U8, "tab_s")
+        tab2_w = [held([P, T3], I32, "tab2_w%d" % a) for a in range(2)]
+        tab2_s = held([P, T3], U8, "tab2_s")
+        w4_raw = held([P, 2, 2 * H], U8, "w4_raw")
+        w4_sraw = held([P, 2, H], U8, "w4_sraw")
+        w4_w = [held([P, 2 * H], U8, "w4_w%d" % a) for a in range(2)]
+        w4_s = [held([P, H], U8, "w4_s%d" % a) for a in range(2)]
+        w1_raw = {(a, b): held([P, PACK, PASS], F32, "w1_raw%d%d" % (a, b)) for a in range(2) for b in range(2)}
+        w1_w = {(a, b): held([P, PASS], U32, "w1_w%d%d" % (a, b)) for a in range(2) for b in range(2)}
+        w1_s = {(a, b): held([P, PASS], U8, "w1_s%d%d" % (a, b)) for a in range(2) for b in range(2)}
+        v_w = [held([P, S], U32, "v_w%d" % a) for a in range(2)]
+        v_s = [held([P, S], U8, "v_s%d" % a) for a in range(2)]
+        v2_w = [held([P, S2], U32, "v2_w%d" % a) for a in range(2)]
+        v2_s = held([P, S2], U8, "v2_s")
+        gain_t = held([P, 2, PACK], F32, "gain_t")
+        open_t = held([P, 2, PACK], F32, "open_t")
+        cue_t = held([P, 4, P2], F32, "cue_t")
+        x_w = {(i, b): held([P, P2], U32, "x_w%d%d" % (i, b)) for i in range(2) for b in range(2)}
+        x_s = {(i, b): held([P, P2], U8, "x_s%d%d" % (i, b)) for i in range(2) for b in range(2)}
+
+        def bank(n):
+            return psum.tile([P, BANK], F32, name="bank%d" % n)
+
+        nc.vector.memset(tab_s[:].rearrange("p a t -> p (a t)").bitcast(I32), 0)
+        nc.vector.memset(w4_sraw[:].rearrange("p a t -> p (a t)").bitcast(I32), 0)
+        nc.vector.memset(tab2_s[:].bitcast(I32), 0)
+
+        def load_w1(a, b):
+            rows = w1[PASS * a : PASS * (a + 1), PASS * b : PASS * (b + 1)]
+            nc.sync.dma_start(w1_raw[a, b][:], rows.rearrange("(p j) c -> p j c", j=PACK))
+
+        def load_words(tile, words):
+            nc.sync.dma_start(tile[:], words.rearrange("p n t -> p (n t)").bitcast(I32))
+
+        nc.sync.dma_start(offs_t[:], offs)
+        load_w1(0, 0)
+        for q in range(4):
+            nc.sync.dma_start(
+                tab_s[32 * q : 32 * q + 4, :, :].bitcast(I32),
+                tab_scales[:, 4 * q : 4 * q + 4, :].rearrange("a r t -> r a t").bitcast(I32),
+            )
+        load_w1(1, 0)
+        load_words(tab_w[0], tab_words[0])
+        for q in range(4):
+            nc.sync.dma_start(
+                w4_sraw[32 * q : 32 * q + 4, :, :].bitcast(I32),
+                w4_scales[:, 4 * q : 4 * q + 4, :].rearrange("a r t -> r a t").bitcast(I32),
+            )
+        nc.sync.dma_start(w4_raw[:].bitcast(I32), w4_words.rearrange("a p c -> p a c").bitcast(I32))
+        load_words(tab_w[1], tab_words[1])
+        nc.sync.dma_start(pos_t[0][:], pos1)
+        nc.sync.dma_start(pos_t[1][:], pos2)
+        nc.sync.dma_start(gain_t[:], gain.rearrange("(b p t) -> p b t", b=2, t=PACK))
+        nc.sync.dma_start(open_t[:], opening.rearrange("(b p t) -> p b t", b=2, t=PACK))
+        load_w1(0, 1)
+        load_w1(1, 1)
+        nc.sync.dma_start(offs2_t[:], offs2)
+        for q in range(4):
+            nc.sync.dma_start(
+                tab2_s[32 * q : 32 * q + 8, :].bitcast(I32),
+                tab2_scales[:, 4 * q : 4 * q + 4, :].bitcast(I32),
+            )
+        load_words(tab2_w[0], tab2_words[0])
+        load_words(tab2_w[1], tab2_words[1])
+        nc.sync.dma_start(cue_t[:], cue.rearrange("(m p) n -> p m n", p=P))
+
+        w1_bf = {}
+
+        def round_w1(a, b, half):
+            if half == 0:
+                w1_bf[a, b] = ring.tile([P, PACK, P, PACK], BF16, name="w1_bf", bufs=2, align_bytes=64)
+            ms = slice(64 * half, 64 * (half + 1))
+            nc.scalar.activation(
+                w1_bf[a, b][:, :, ms, :].rearrange("p t m j -> p m j t"),
+                w1_raw[a, b][:].rearrange("p j (m t) -> p m j t", t=PACK)[:, ms, :, :],
+                IDENT,
+            )
+
+        def quantise_w1(a, b):
+            nc.vector.quantize_mx(
+                out=w1_w[a, b][:].bitcast(FP8X4), scales=w1_s[a, b][:],
+                in_=w1_bf[a, b][:].rearrange("p t m j -> p (t m j)"),
+            )
+
+        def deal_w4_words(a):
+            nc.vector.tensor_copy(
+                w4_w[a][:].bitcast(U16).rearrange("p (b t g i) -> p b g t i", b=2, t=PACK, i=8),
+                w4_raw[:, a, :].bitcast(U16).rearrange("p (b g i t) -> p b g t i", b=2, t=PACK, i=8),
+            )
+
+        def deal_w4_scales(a):
+            nc.vector.tensor_copy(
+                w4_s[a][:].rearrange("p (b t g i) -> p b g t i", b=2, t=PACK, i=16),
+                w4_sraw[:, a, :].rearrange("p (b g i t) -> p b g t i", b=2, t=PACK, i=16),
+            )
+
+        def gather_v_words(a, lo, hi):
+            nc.vector.tensor_copy(v_w[a][:, lo:hi], tab_w[a][:].bitcast(U32).indirect(offs_t[:, lo // 16 : hi // 16]))
+
+        banks = {}
+
+        def first_pass(i, a, half):
+            b, t = divmod(i, PACK)
+            if a == 0:
+                banks[i, half, "own"] = bank(4 * (i % 2) + 2 * half)
+                banks[i, half, "other"] = bank(4 * (i % 2) + 2 * half + 1)
+            cols = slice(BANK * half, BANK * (half + 1))
+            c0 = PASS * b + P * t
+            nc.tensor.matmul_mx(
+                banks[i, half, "other"][:], lhsT=w4_w[a][:, 2 * c0 : 2 * (c0 + P)].bitcast(FP4X4),
+                lhsT_scale=w4_s[a][:, c0 : c0 + P], rhs=v_w[a][:, cols].bitcast(FP8X4),
+                rhs_scale=v_s[a][:, cols], start=(a == 0), stop=(a == 1),
+            )
+            nc.tensor.matmul_mx(
+                banks[i, half, "own"][:], lhsT=w1_w[a, b][:, P * t : P * (t + 1)].bitcast(FP8X4),
+                lhsT_scale=w1_s[a, b][:, P * t : P * (t + 1)], rhs=v_w[a][:, cols].bitcast(FP8X4),
+                rhs_scale=v_s[a][:, cols], start=(a == 0), stop=(a == 1),
+            )
+
+        def multiply(i):
+            for half in range(2):
+                for a in range(2):
+                    first_pass(i, a, half)
+
+        others = {}
+        top = {}
+
+        def fetch_other(i):
+            for half in range(2):
+                others[i, half] = ring.tile([P, BANK], F32, name="other", bufs=4, align_bytes=64)
+                nc.scalar.copy(others[i, half][:], banks[i, half, "other"][:])
+
+        def take_max(i):
+            top[i] = ring.tile([P, S], F32, name="top", bufs=4, align_bytes=64)
+            for half in range(2):
+                nc.vector.tensor_tensor(
+                    top[i][:, BANK * half : BANK * (half + 1)], banks[i, half, "own"][:], others[i, half][:], ALU.max
+                )
+
+        picked = {}
+
+        def pick(i, lst):
+            picked[i, lst] = ring.tile([P, P2], F32, name="picked", bufs=8, align_bytes=64)
+            nc.vector.tensor_copy(picked[i, lst][:], top[i][:].indirect(pos_t[lst][:]))
+
+        rows_bf = {}
+        woven = {}
+
+        def round_x(i, lst):
+            b, t = divmod(i, PACK)
+            if t == 0:
+                rows_bf[lst, b] = ring.tile([P, PACK, P2], BF16, name="rows_bf", bufs=4, align_bytes=64)
+            bias = open_t[:, b, t : t + 1] if lst == 0 else 0.0
+            nc.scalar.activation(rows_bf[lst, b][:, t, :], picked[i, lst][:], IDENT, bias=bias, scale=gain_t[:, b, t : t + 1])
+
+        def weave(lst, b, lo, hi):
+            if lo == 0:
+                woven[lst, b] = ring.tile([P, P2, PACK], BF16, name="woven", bufs=2, align_bytes=64)
+            nc.scalar.copy(
+                woven[lst, b][:, lo:hi, :].rearrange("p (c i) t -> p c t i", i=4),
+                rows_bf[lst, b][:, :, lo:hi].rearrange("p t (c i) -> p c t i", i=4),
+            )
+
+        def quantise_x(lst, b, lo, hi):
+            nc.vector.quantize_mx(
+                out=x_w[lst, b][:, lo:hi].bitcast(FP8X4), scales=x_s[lst, b][:, lo:hi],
+                in_=woven[lst, b][:, lo:hi, :].rearrange("p n t -> p (n t)"),
+            )
+
+        def second_pass(dst, lst, b, m, lo, hi, start, stop):
+            nc.tensor.matmul_mx(
+                dst, lhsT=v2_w[b][:, P * m : P * (m + 1)].bitcast(FP8X4),
+                lhsT_scale=v2_s[4 * b : P, P * m : P * (m + 1)], rhs=x_w[lst, b][:, lo:hi].bitcast(FP8X4),
+                rhs_scale=x_s[lst, b][:, lo:hi], start=start, stop=stop,
+            )
+
+        for a in range(2):
+            nc.vector.tensor_copy(v_s[a][:], tab_s[:, a, :].indirect(offs_t[:]))
+        for a in range(2):
+            round_w1(a, 0, 0)
+            round_w1(a, 0, 1)
+        for a in range(2):
+            quantise_w1(a, 0)
+        gather_v_words(0, 0, S)
+        for a in range(2):
+            deal_w4_scales(a)
+            deal_w4_words(a)
+        for i in range(2):
+            for half in range(2):
+                first_pass(i, 0, half)
+        for half in range(2):
+            gather_v_words(1, BANK * half, BANK * (half + 1))
+            for i in range(2):
+                first_pass(i, 1, half)
+        fetch_other(0)
+        fetch_other(1)
+
+        for i in range(4):
+            take_max(i)
+            if i == 2:
+                quantise_w1(0, 1)
+                quantise_w1(1, 1)
+            multiply(i + 2)
+            pick(i, 0)
+            pick(i, 1)
+            if i < 2:
+                round_w1(i, 1, 0)
+                round_w1(i, 1, 1)
+            fetch_other(i + 2)
+            if i >= 2:
+                for j in (2 * (i - 2), 2 * (i - 2) + 1):
+                    round_x(j, 0)
+                    round_x(j, 1)
+
+        e1 = []
+        e2 = {}
+        for i in range(4, 8):
+            take_max(i)
+            if i < 6:
+                multiply(i + 2)
+            pick(i, 0)
+            if i < 6:
+                fetch_other(i + 2)
+            round_x(i, 0)
+            if i == 4:
+                nc.vector.tensor_copy(v2_s[:], tab2_s[:].indirect(offs2_t[:]))
+                weave(0, 0, 0, 256)
+                weave(0, 0, 256, 512)
+            if i == 5:
+                nc.vector.tensor_copy(v2_w[0][:], tab2_w[0][:].bitcast(U32).indirect(offs2_t[:]))
+                quantise_x(0, 0, 0, P2)
+                weave(1, 0, 0, 256)
+                weave(1, 0, 256, 512)
+            if i == 6:
+                nc.vector.tensor_copy(v2_w[1][:], tab2_w[1][:].bitcast(U32).indirect(offs2_t[:]))
+                quantise_x(1, 0, 0, P2)
+                for m in range(4):
+                    e1.append(bank(m))
+                    second_pass(e1[m][:], 0, 0, m, 0, P2, True, False)
+            if i == 7:
+                for half in range(2):
+                    for pair in range(2):
+                        e2[half, pair] = bank(4 + 2 * half + pair)
+                        for mm in range(2):
+                            second_pass(e2[half, pair][:, 256 * mm : 256 * (mm + 1)], 1, 0, 2 * pair + mm,
+                                        256 * half, 256 * (half + 1), mm == 0, False)
+        weave(0, 1, 0, 256)
+        weave(0, 1, 256, 512)
+        for i in range(4, 7):
+            pick(i, 1)
+            round_x(i, 1)
+        quantise_x(0, 1, 0, P2)
+        for m in range(4):
+            second_pass(e1[m][:], 0, 1, m, 0, P2, False, True)
+        pick(7, 1)
+        round_x(7, 1)
+        weave(1, 1, 0, 256)
+        weave(1, 1, 256, 512)
+        for m in range(4):
+            nc.vector.tensor_tensor(cue_t[:, m, :], e1[m][:], cue_t[:, m, :], ALU.mult)
+        for half in range(2):
+            quantise_x(1, 1, 256 * half, 256 * (half + 1))
+            for pair in range(2):
+                for mm in range(2):
+                    second_pass(e2[half, pair][:, 256 * mm : 256 * (mm + 1)], 1, 1, 2 * pair + mm,
+                                256 * half, 256 * (half + 1), False, mm == 1)
+        out_v = out.rearrange("(m p) n -> p m n", p=P)
+        for half in range(2):
+            for pair in range(2):
+                part = cue_t[:, 2 * pair : 2 * pair + 2, 256 * half : 256 * (half + 1)]
+                nc.vector.tensor_tensor(part, e2[half, pair][:].rearrange("p (m n) -> p m n", m=2), part, ALU.mult)
+                nc.sync.dma_start(out_v[:, 2 * pair : 2 * pair + 2, 256 * half : 256 * (half + 1)], part)

@@ -39,19 +39,21 @@ def tile_list_runway_look_order_kernel(
         offs2_t = held([P, S2 // 16], U16, "offs2_t")
         pos_t = [held([P, P2 // 16], U16, "pos%d_t" % i) for i in range(2)]
         tab_w = [held([P, T], I32, "tab_w%d" % a) for a in range(2)]
-        tab_s = held([P, 2, T], U8, "tab_s")
+        tab_s = held([P, T], U8, "tab_s")
+        v_rows = held([P, S], U8, "v_rows")
         tab2_w = [held([P, T3], I32, "tab2_w%d" % a) for a in range(2)]
         tab2_s = held([P, T3], U8, "tab2_s")
         w4_raw = held([P, 2, 2 * H], U8, "w4_raw")
         w4_sraw = held([P, 2, H], U8, "w4_sraw")
         w4_w = [held([P, 2 * H], U8, "w4_w%d" % a) for a in range(2)]
-        w4_s = [held([P, H], U8, "w4_s%d" % a) for a in range(2)]
-        w1_raw = {(a, b): held([P, PACK, PASS], F32, "w1_raw%d%d" % (a, b)) for a in range(2) for b in range(2)}
-        w1_w = {(a, b): held([P, PASS], U32, "w1_w%d%d" % (a, b)) for a in range(2) for b in range(2)}
+        w4_s = {0: held([P, 2, PASS], U8, "w4_s0")}
+        w1_raw = {(a, b): held([P, PACK, PASS], F32, "w1_raw%d%d" % (a, b)) for a, b in ((0, 0), (0, 1), (1, 1))}
+        w1_last = [held([P, PACK, PASS // 2], F32, "w1_last%d" % half) for half in range(2)]
+        w1_w = {(a, b): held([P, PASS], U32, "w1_w%d%d" % (a, b)) for a, b in ((0, 1), (1, 0), (1, 1))}
         w1_s = {(a, b): held([P, PASS], U8, "w1_s%d%d" % (a, b)) for a in range(2) for b in range(2)}
         v_w = [held([P, S], U32, "v_w%d" % a) for a in range(2)]
         v_s = [held([P, S], U8, "v_s%d" % a) for a in range(2)]
-        v2_w = [held([P, S2], U32, "v2_w%d" % a) for a in range(2)]
+        v2_w = {0: held([P, S2], U32, "v2_w0")}
         v2_s = held([P, S2], U8, "v2_s")
         gain_t = held([P, 2, PACK], F32, "gain_t")
         open_t = held([P, 2, PACK], F32, "open_t")
@@ -62,9 +64,18 @@ def tile_list_runway_look_order_kernel(
         def bank(n):
             return psum.tile([P, BANK], F32, name="bank%d" % n)
 
-        nc.vector.memset(tab_s[:].rearrange("p a t -> p (a t)").bitcast(I32), 0)
         nc.vector.memset(w4_sraw[:].rearrange("p a t -> p (a t)").bitcast(I32), 0)
+        nc.vector.memset(tab_s[:].bitcast(I32), 0)
+        for a in range(2):
+            nc.vector.memset(v_s[a][:].bitcast(I32), 0)
         nc.vector.memset(tab2_s[:].bitcast(I32), 0)
+
+        def load_planes(tile, scales):
+            for r in range(4):
+                nc.sync.dma_start(
+                    tile[r:P:32, :, :].bitcast(I32),
+                    scales[:, r:16:4, :].rearrange("a q t -> q a t").bitcast(I32),
+                )
 
         def load_w1(a, b):
             rows = w1[PASS * a : PASS * (a + 1), PASS * b : PASS * (b + 1)]
@@ -74,27 +85,21 @@ def tile_list_runway_look_order_kernel(
             nc.sync.dma_start(tile[:], words.rearrange("p n t -> p (n t)").bitcast(I32))
 
         nc.sync.dma_start(offs_t[:], offs)
-        load_w1(0, 0)
-        for q in range(4):
-            nc.sync.dma_start(
-                tab_s[32 * q : 32 * q + 4, :, :].bitcast(I32),
-                tab_scales[:, 4 * q : 4 * q + 4, :].rearrange("a r t -> r a t").bitcast(I32),
-            )
-        load_w1(1, 0)
-        load_words(tab_w[0], tab_words[0])
-        for q in range(4):
-            nc.sync.dma_start(
-                w4_sraw[32 * q : 32 * q + 4, :, :].bitcast(I32),
-                w4_scales[:, 4 * q : 4 * q + 4, :].rearrange("a r t -> r a t").bitcast(I32),
-            )
         nc.sync.dma_start(w4_raw[:].bitcast(I32), w4_words.rearrange("a p c -> p a c").bitcast(I32))
+        load_planes(w4_sraw, w4_scales)
+        nc.sync.dma_start(tab_s[0:P:4, :].bitcast(I32), tab_scales.rearrange("a q t -> (a q) t").bitcast(I32))
+        load_w1(0, 0)
+        load_words(tab_w[0], tab_words[0])
         load_words(tab_w[1], tab_words[1])
+        for half in range(2):
+            rows = w1[PASS:K, 256 * half : 256 * (half + 1)]
+            nc.sync.dma_start(w1_last[half][:], rows.rearrange("(p j) c -> p j c", j=PACK))
         nc.sync.dma_start(pos_t[0][:], pos1)
         nc.sync.dma_start(pos_t[1][:], pos2)
         nc.sync.dma_start(gain_t[:], gain.rearrange("(b p t) -> p b t", b=2, t=PACK))
-        nc.sync.dma_start(open_t[:], opening.rearrange("(b p t) -> p b t", b=2, t=PACK))
         load_w1(0, 1)
         load_w1(1, 1)
+        nc.sync.dma_start(open_t[:], opening.rearrange("(b p t) -> p b t", b=2, t=PACK))
         nc.sync.dma_start(offs2_t[:], offs2)
         for q in range(4):
             nc.sync.dma_start(
@@ -112,8 +117,8 @@ def tile_list_runway_look_order_kernel(
                 w1_bf[a, b] = ring.tile([P, PACK, P, PACK], BF16, name="w1_bf", bufs=2, align_bytes=64)
             ms = slice(64 * half, 64 * (half + 1))
             nc.scalar.activation(
-                w1_bf[a, b][:, :, ms, :].rearrange("p t m j -> p m j t"),
-                w1_raw[a, b][:].rearrange("p j (m t) -> p m j t", t=PACK)[:, ms, :, :],
+                w1_bf[a, b][:, :, ms, :].rearrange("p t m j -> p m t j"),
+                w1_raw[a, b][:].rearrange("p j (m t) -> p m t j", t=PACK)[:, ms, :, :],
                 IDENT,
             )
 
@@ -129,10 +134,10 @@ def tile_list_runway_look_order_kernel(
                 w4_raw[:, a, :].bitcast(U16).rearrange("p (b g i t) -> p b g t i", b=2, t=PACK, i=8),
             )
 
-        def deal_w4_scales(a):
+        def deal_w4_scales(b):
             nc.vector.tensor_copy(
-                w4_s[a][:].rearrange("p (b t g i) -> p b g t i", b=2, t=PACK, i=16),
-                w4_sraw[:, a, :].rearrange("p (b g i t) -> p b g t i", b=2, t=PACK, i=16),
+                w4_s[b][:].rearrange("p a (t g i) -> p a g t i", t=PACK, i=16),
+                w4_sraw[:, :, PASS * b : PASS * (b + 1)].rearrange("p a (g i t) -> p a g t i", t=PACK, i=16),
             )
 
         def gather_v_words(a, lo, hi):
@@ -140,23 +145,25 @@ def tile_list_runway_look_order_kernel(
 
         banks = {}
 
-        def first_pass(i, a, half):
+        def first_pass(i, a, half, kinds=("other", "own")):
             b, t = divmod(i, PACK)
             if a == 0:
                 banks[i, half, "own"] = bank(4 * (i % 2) + 2 * half)
                 banks[i, half, "other"] = bank(4 * (i % 2) + 2 * half + 1)
             cols = slice(BANK * half, BANK * (half + 1))
             c0 = PASS * b + P * t
-            nc.tensor.matmul_mx(
-                banks[i, half, "other"][:], lhsT=w4_w[a][:, 2 * c0 : 2 * (c0 + P)].bitcast(FP4X4),
-                lhsT_scale=w4_s[a][:, c0 : c0 + P], rhs=v_w[a][:, cols].bitcast(FP8X4),
-                rhs_scale=v_s[a][:, cols], start=(a == 0), stop=(a == 1),
-            )
-            nc.tensor.matmul_mx(
-                banks[i, half, "own"][:], lhsT=w1_w[a, b][:, P * t : P * (t + 1)].bitcast(FP8X4),
-                lhsT_scale=w1_s[a, b][:, P * t : P * (t + 1)], rhs=v_w[a][:, cols].bitcast(FP8X4),
-                rhs_scale=v_s[a][:, cols], start=(a == 0), stop=(a == 1),
-            )
+            if "other" in kinds:
+                nc.tensor.matmul_mx(
+                    banks[i, half, "other"][:], lhsT=w4_w[a][:, 2 * c0 : 2 * (c0 + P)].bitcast(FP4X4),
+                    lhsT_scale=w4_s[b][:, a, P * t : P * (t + 1)], rhs=v_w[a][:, cols].bitcast(FP8X4),
+                    rhs_scale=v_s[a][:, cols], start=(a == 0), stop=(a == 1),
+                )
+            if "own" in kinds:
+                nc.tensor.matmul_mx(
+                    banks[i, half, "own"][:], lhsT=w1_w[a, b][:, P * t : P * (t + 1)].bitcast(FP8X4),
+                    lhsT_scale=w1_s[a, b][:, P * t : P * (t + 1)], rhs=v_w[a][:, cols].bitcast(FP8X4),
+                    rhs_scale=v_s[a][:, cols], start=(a == 0), stop=(a == 1),
+                )
 
         def multiply(i):
             for half in range(2):
@@ -166,37 +173,52 @@ def tile_list_runway_look_order_kernel(
         others = {}
         top = {}
 
+        def other_slot(i, half):
+            return "front%d" % (i % 3) if half == 0 else "back%d" % (i % 2)
+
         def fetch_other(i):
+            if i == 0:
+                others["first"] = keep.tile([P, 2 * S], F32, name="w1_last0", align_bytes=64)
             for half in range(2):
-                others[i, half] = ring.tile([P, BANK], F32, name="other", bufs=4, align_bytes=64)
-                nc.scalar.copy(others[i, half][:], banks[i, half, "other"][:])
+                if i < 2:
+                    others[i, half] = others["first"][:, S * i + BANK * half : S * i + BANK * (half + 1)]
+                else:
+                    others[i, half] = keep.tile([P, BANK], F32, name=other_slot(i, half), align_bytes=64)[:]
+                nc.scalar.copy(others[i, half], banks[i, half, "other"][:])
 
         def take_max(i):
             top[i] = ring.tile([P, S], F32, name="top", bufs=4, align_bytes=64)
             for half in range(2):
                 nc.vector.tensor_tensor(
-                    top[i][:, BANK * half : BANK * (half + 1)], banks[i, half, "own"][:], others[i, half][:], ALU.max
+                    top[i][:, BANK * half : BANK * (half + 1)], banks[i, half, "own"][:], others[i, half], ALU.max
                 )
 
         picked = {}
 
-        def pick(i, lst):
-            picked[i, lst] = ring.tile([P, P2], F32, name="picked", bufs=8, align_bytes=64)
-            nc.vector.tensor_copy(picked[i, lst][:], top[i][:].indirect(pos_t[lst][:]))
+        def pick(i, lst, slot=None, parts=1):
+            if slot is None:
+                picked[i, lst] = ring.tile([P, P2], F32, name="picked", bufs=5, align_bytes=64)
+            else:
+                picked[i, lst] = keep.tile([P, P2], F32, name=slot, align_bytes=64)
+            width = P2 // parts
+            for lo in range(0, P2, width):
+                offsets = pos_t[lst][:, lo // 16 : (lo + width) // 16]
+                nc.vector.tensor_copy(picked[i, lst][:, lo : lo + width], top[i][:].indirect(offsets))
 
         rows_bf = {}
         woven = {}
 
-        def round_x(i, lst):
+        def round_x(i, lst, lo=0, hi=P2):
             b, t = divmod(i, PACK)
             if t == 0:
                 rows_bf[lst, b] = ring.tile([P, PACK, P2], BF16, name="rows_bf", bufs=4, align_bytes=64)
             bias = open_t[:, b, t : t + 1] if lst == 0 else 0.0
-            nc.scalar.activation(rows_bf[lst, b][:, t, :], picked[i, lst][:], IDENT, bias=bias, scale=gain_t[:, b, t : t + 1])
+            scale = gain_t[:, b, t : t + 1]
+            nc.scalar.activation(rows_bf[lst, b][:, t, lo:hi], picked[i, lst][:, lo:hi], IDENT, bias=bias, scale=scale)
 
         def weave(lst, b, lo, hi):
             if lo == 0:
-                woven[lst, b] = ring.tile([P, P2, PACK], BF16, name="woven", bufs=2, align_bytes=64)
+                woven[lst, b] = keep.tile([P, P2, PACK], BF16, name="woven%d" % lst, align_bytes=64)
             nc.scalar.copy(
                 woven[lst, b][:, lo:hi, :].rearrange("p (c i) t -> p c t i", i=4),
                 rows_bf[lst, b][:, :, lo:hi].rearrange("p t (c i) -> p c t i", i=4),
@@ -215,43 +237,75 @@ def tile_list_runway_look_order_kernel(
                 rhs_scale=x_s[lst, b][:, lo:hi], start=start, stop=stop,
             )
 
+        nc.vector.tensor_copy(v_rows[:], tab_s[:].indirect(offs_t[:]))
         for a in range(2):
-            nc.vector.tensor_copy(v_s[a][:], tab_s[:, a, :].indirect(offs_t[:]))
-        for a in range(2):
-            round_w1(a, 0, 0)
-            round_w1(a, 0, 1)
-        for a in range(2):
-            quantise_w1(a, 0)
-        gather_v_words(0, 0, S)
-        for a in range(2):
-            deal_w4_scales(a)
             deal_w4_words(a)
+        deal_w4_scales(0)
+        round_w1(0, 0, 0)
+        round_w1(0, 0, 1)
+        for a in range(2):
+            for r in range(4):
+                nc.scalar.dma_start(
+                    v_s[a][r:P:32, :].bitcast(I32), v_rows[64 * a + 4 * r : 64 * (a + 1) : 16, :].bitcast(I32)
+                )
+        w1_w[0, 0] = held([P, PASS], U32, "tab_s")
+        quantise_w1(0, 0)
+        gather_v_words(0, 0, S)
         for i in range(2):
             for half in range(2):
                 first_pass(i, 0, half)
         for half in range(2):
             gather_v_words(1, BANK * half, BANK * (half + 1))
-            for i in range(2):
-                first_pass(i, 1, half)
+            first_pass(0, 1, half, ("other",))
+        for half in range(2):
+            first_pass(1, 1, half, ("other",))
+        last_bf = [held([P, 2, P, PACK], BF16, "last_bf%d" % pair) for pair in range(2)]
+        last_out = [last_bf[pair][:].rearrange("p t m j -> p m t j") for pair in range(2)]
+        last_in = [w1_last[half][:].rearrange("p j (m t) -> p m t j", t=PACK) for half in range(2)]
+
+        def quantise_last(pair):
+            cols = slice(256 * pair, 256 * (pair + 1))
+            nc.vector.quantize_mx(
+                out=w1_w[1, 0][:, cols].bitcast(FP8X4), scales=w1_s[1, 0][:, cols],
+                in_=last_bf[pair][:].rearrange("p t m j -> p (t m j)"),
+            )
+
+        for pair in range(2):
+            nc.scalar.activation(last_out[pair][:, 0:64, :, :], last_in[0][:, :, 2 * pair : 2 * pair + 2, :], IDENT)
+        nc.vector.tensor_copy(last_out[0][:, 64:P, :, :], last_in[1][:, :, 0:2, :])
+        quantise_last(0)
+        for i in range(2):
+            for half in range(2):
+                first_pass(i, 1, half, ("own",))
         fetch_other(0)
         fetch_other(1)
+        nc.scalar.activation(last_out[1][:, 64:P, :, :], last_in[1][:, :, 2:4, :], IDENT)
+        w4_s[1] = held([P, 2, PASS], U8, "last_bf0")
+        deal_w4_scales(1)
 
         for i in range(4):
             take_max(i)
+            if i == 0:
+                quantise_last(1)
             if i == 2:
                 quantise_w1(0, 1)
                 quantise_w1(1, 1)
             multiply(i + 2)
+            if i > 0:
+                pick(i - 1, 1, "w1_last0" if i == 1 else other_slot(i, 0))
             pick(i, 0)
-            pick(i, 1)
             if i < 2:
                 round_w1(i, 1, 0)
                 round_w1(i, 1, 1)
             fetch_other(i + 2)
-            if i >= 2:
-                for j in (2 * (i - 2), 2 * (i - 2) + 1):
+            if i == 2:
+                for j in range(2):
                     round_x(j, 0)
                     round_x(j, 1)
+            if i == 3:
+                round_x(2, 0)
+                round_x(2, 1)
+                round_x(3, 0)
 
         e1 = []
         e2 = {}
@@ -259,44 +313,46 @@ def tile_list_runway_look_order_kernel(
             take_max(i)
             if i < 6:
                 multiply(i + 2)
-            pick(i, 0)
-            if i < 6:
                 fetch_other(i + 2)
-            round_x(i, 0)
             if i == 4:
-                nc.vector.tensor_copy(v2_s[:], tab2_s[:].indirect(offs2_t[:]))
+                pick(3, 1, other_slot(4, 0))
+                round_x(3, 1)
                 weave(0, 0, 0, 256)
                 weave(0, 0, 256, 512)
             if i == 5:
-                nc.vector.tensor_copy(v2_w[0][:], tab2_w[0][:].bitcast(U32).indirect(offs2_t[:]))
+                nc.vector.tensor_copy(v2_s[:], tab2_s[:].indirect(offs2_t[:]))
                 quantise_x(0, 0, 0, P2)
                 weave(1, 0, 0, 256)
                 weave(1, 0, 256, 512)
             if i == 6:
-                nc.vector.tensor_copy(v2_w[1][:], tab2_w[1][:].bitcast(U32).indirect(offs2_t[:]))
+                nc.vector.tensor_copy(v2_w[0][:], tab2_w[0][:].bitcast(U32).indirect(offs2_t[:]))
                 quantise_x(1, 0, 0, P2)
                 for m in range(4):
                     e1.append(bank(m))
                     second_pass(e1[m][:], 0, 0, m, 0, P2, True, False)
             if i == 7:
+                v2_w[1] = held([P, S2], U32, other_slot(7, 0))
+                nc.vector.tensor_copy(v2_w[1][:], tab2_w[1][:].bitcast(U32).indirect(offs2_t[:]))
                 for half in range(2):
                     for pair in range(2):
                         e2[half, pair] = bank(4 + 2 * half + pair)
                         for mm in range(2):
                             second_pass(e2[half, pair][:, 256 * mm : 256 * (mm + 1)], 1, 0, 2 * pair + mm,
                                         256 * half, 256 * (half + 1), mm == 0, False)
+            pick(i, 0, "late" if i == 7 else None)
+            round_x(i, 0)
         weave(0, 1, 0, 256)
         weave(0, 1, 256, 512)
         for i in range(4, 7):
-            pick(i, 1)
+            pick(i, 1, (other_slot(7, 1), "late", "tab2_w1")[i - 4])
             round_x(i, 1)
         quantise_x(0, 1, 0, P2)
         for m in range(4):
             second_pass(e1[m][:], 0, 1, m, 0, P2, False, True)
-        pick(7, 1)
-        round_x(7, 1)
-        weave(1, 1, 0, 256)
-        weave(1, 1, 256, 512)
+        pick(7, 1, "woven0", parts=2)
+        for lo in (0, 256):
+            round_x(7, 1, lo, lo + 256)
+            weave(1, 1, lo, lo + 256)
         for m in range(4):
             nc.vector.tensor_tensor(cue_t[:, m, :], e1[m][:], cue_t[:, m, :], ALU.mult)
         for half in range(2):

@@ -43,10 +43,10 @@ def tile_list_runway_look_order_kernel(
         v_rows = held([P, S], U8, "v_rows")
         tab2_w = [held([P, T3], I32, "tab2_w%d" % a) for a in range(2)]
         tab2_s = held([P, T3], U8, "tab2_s")
-        w4_raw = held([P, 2, 2 * H], U8, "w4_raw")
+        w4_raw = [held([P, 2, H], U8, "w4_raw%d" % b) for b in range(2)]
         w4_sraw = held([P, 2, H], U8, "w4_sraw")
-        w4_w = [held([P, 2 * H], U8, "w4_w%d" % a) for a in range(2)]
-        w4_s = {0: held([P, 2, PASS], U8, "w4_s0")}
+        w4_w = [held([P, 2, H], U8, "w4_w%d" % b) for b in range(2)]
+        w4_s = [held([P, 2, PASS], U8, "w4_s%d" % b) for b in range(2)]
         w1_raw = {(a, b): held([P, PACK, PASS], F32, "w1_raw%d%d" % (a, b)) for a, b in ((0, 0), (0, 1), (1, 1))}
         w1_last = [held([P, PACK, PASS // 2], F32, "w1_last%d" % half) for half in range(2)]
         w1_w = {(a, b): held([P, PASS], U32, "w1_w%d%d" % (a, b)) for a, b in ((0, 1), (1, 0), (1, 1))}
@@ -81,11 +81,15 @@ def tile_list_runway_look_order_kernel(
             rows = w1[PASS * a : PASS * (a + 1), PASS * b : PASS * (b + 1)]
             nc.sync.dma_start(w1_raw[a, b][:], rows.rearrange("(p j) c -> p j c", j=PACK))
 
+        def load_w4_words(b):
+            part = w4_words[:, :, H * b : H * (b + 1)]
+            nc.sync.dma_start(w4_raw[b][:].bitcast(I32), part.rearrange("a p c -> p a c").bitcast(I32))
+
         def load_words(tile, words):
             nc.sync.dma_start(tile[:], words.rearrange("p n t -> p (n t)").bitcast(I32))
 
         nc.sync.dma_start(offs_t[:], offs)
-        nc.sync.dma_start(w4_raw[:].bitcast(I32), w4_words.rearrange("a p c -> p a c").bitcast(I32))
+        load_w4_words(0)
         load_planes(w4_sraw, w4_scales)
         nc.sync.dma_start(tab_s[0:P:4, :].bitcast(I32), tab_scales.rearrange("a q t -> (a q) t").bitcast(I32))
         load_w1(0, 0)
@@ -94,6 +98,7 @@ def tile_list_runway_look_order_kernel(
         for half in range(2):
             rows = w1[PASS:K, 256 * half : 256 * (half + 1)]
             nc.sync.dma_start(w1_last[half][:], rows.rearrange("(p j) c -> p j c", j=PACK))
+        load_w4_words(1)
         nc.sync.dma_start(pos_t[0][:], pos1)
         nc.sync.dma_start(pos_t[1][:], pos2)
         nc.sync.dma_start(gain_t[:], gain.rearrange("(b p t) -> p b t", b=2, t=PACK))
@@ -128,10 +133,10 @@ def tile_list_runway_look_order_kernel(
                 in_=w1_bf[a, b][:].rearrange("p t m j -> p (t m j)"),
             )
 
-        def deal_w4_words(a):
+        def deal_w4_words(b):
             nc.vector.tensor_copy(
-                w4_w[a][:].bitcast(U16).rearrange("p (b t g i) -> p b g t i", b=2, t=PACK, i=8),
-                w4_raw[:, a, :].bitcast(U16).rearrange("p (b g i t) -> p b g t i", b=2, t=PACK, i=8),
+                w4_w[b][:].bitcast(U16).rearrange("p a (t g i) -> p a g t i", t=PACK, i=8),
+                w4_raw[b][:].bitcast(U16).rearrange("p a (g i t) -> p a g t i", t=PACK, i=8),
             )
 
         def deal_w4_scales(b):
@@ -151,10 +156,9 @@ def tile_list_runway_look_order_kernel(
                 banks[i, half, "own"] = bank(4 * (i % 2) + 2 * half)
                 banks[i, half, "other"] = bank(4 * (i % 2) + 2 * half + 1)
             cols = slice(BANK * half, BANK * (half + 1))
-            c0 = PASS * b + P * t
             if "other" in kinds:
                 nc.tensor.matmul_mx(
-                    banks[i, half, "other"][:], lhsT=w4_w[a][:, 2 * c0 : 2 * (c0 + P)].bitcast(FP4X4),
+                    banks[i, half, "other"][:], lhsT=w4_w[b][:, a, 2 * P * t : 2 * P * (t + 1)].bitcast(FP4X4),
                     lhsT_scale=w4_s[b][:, a, P * t : P * (t + 1)], rhs=v_w[a][:, cols].bitcast(FP8X4),
                     rhs_scale=v_s[a][:, cols], start=(a == 0), stop=(a == 1),
                 )
@@ -211,17 +215,17 @@ def tile_list_runway_look_order_kernel(
         def round_x(i, lst, lo=0, hi=P2):
             b, t = divmod(i, PACK)
             if t == 0:
-                rows_bf[lst, b] = ring.tile([P, PACK, P2], BF16, name="rows_bf", bufs=4, align_bytes=64)
+                rows_bf[lst, b] = ring.tile([P, 2, P2, 2], BF16, name="rows_bf", bufs=4, align_bytes=64)
             bias = open_t[:, b, t : t + 1] if lst == 0 else 0.0
             scale = gain_t[:, b, t : t + 1]
-            nc.scalar.activation(rows_bf[lst, b][:, t, lo:hi], picked[i, lst][:, lo:hi], IDENT, bias=bias, scale=scale)
+            nc.scalar.activation(rows_bf[lst, b][:, t // 2, lo:hi, t % 2], picked[i, lst][:, lo:hi], IDENT, bias=bias, scale=scale)
 
         def weave(lst, b, lo, hi):
             if lo == 0:
                 woven[lst, b] = keep.tile([P, P2, PACK], BF16, name="woven%d" % lst, align_bytes=64)
             nc.scalar.copy(
-                woven[lst, b][:, lo:hi, :].rearrange("p (c i) t -> p c t i", i=4),
-                rows_bf[lst, b][:, :, lo:hi].rearrange("p t (c i) -> p c t i", i=4),
+                woven[lst, b][:, lo:hi, :].bitcast(U32),
+                rows_bf[lst, b][:, :, lo:hi, :].bitcast(U32).rearrange("p u n one -> p n (u one)"),
             )
 
         def quantise_x(lst, b, lo, hi):
@@ -238,9 +242,9 @@ def tile_list_runway_look_order_kernel(
             )
 
         nc.vector.tensor_copy(v_rows[:], tab_s[:].indirect(offs_t[:]))
-        for a in range(2):
-            deal_w4_words(a)
+        deal_w4_words(0)
         deal_w4_scales(0)
+        deal_w4_scales(1)
         round_w1(0, 0, 0)
         round_w1(0, 0, 1)
         for a in range(2):
@@ -248,9 +252,9 @@ def tile_list_runway_look_order_kernel(
                 nc.scalar.dma_start(
                     v_s[a][r:P:32, :].bitcast(I32), v_rows[64 * a + 4 * r : 64 * (a + 1) : 16, :].bitcast(I32)
                 )
-        w1_w[0, 0] = held([P, PASS], U32, "tab_s")
-        quantise_w1(0, 0)
         gather_v_words(0, 0, S)
+        w1_w[0, 0] = held([P, PASS], U32, "tab_w0")
+        quantise_w1(0, 0)
         for i in range(2):
             for half in range(2):
                 first_pass(i, 0, half)
@@ -280,8 +284,7 @@ def tile_list_runway_look_order_kernel(
         fetch_other(0)
         fetch_other(1)
         nc.scalar.activation(last_out[1][:, 64:P, :, :], last_in[1][:, :, 2:4, :], IDENT)
-        w4_s[1] = held([P, 2, PASS], U8, "last_bf0")
-        deal_w4_scales(1)
+        deal_w4_words(1)
 
         for i in range(4):
             take_max(i)
@@ -317,13 +320,11 @@ def tile_list_runway_look_order_kernel(
             if i == 4:
                 pick(3, 1, other_slot(4, 0))
                 round_x(3, 1)
-                weave(0, 0, 0, 256)
-                weave(0, 0, 256, 512)
+                weave(0, 0, 0, P2)
             if i == 5:
                 nc.vector.tensor_copy(v2_s[:], tab2_s[:].indirect(offs2_t[:]))
                 quantise_x(0, 0, 0, P2)
-                weave(1, 0, 0, 256)
-                weave(1, 0, 256, 512)
+                weave(1, 0, 0, P2)
             if i == 6:
                 nc.vector.tensor_copy(v2_w[0][:], tab2_w[0][:].bitcast(U32).indirect(offs2_t[:]))
                 quantise_x(1, 0, 0, P2)
@@ -341,8 +342,7 @@ def tile_list_runway_look_order_kernel(
                                         256 * half, 256 * (half + 1), mm == 0, False)
             pick(i, 0, "late" if i == 7 else None)
             round_x(i, 0)
-        weave(0, 1, 0, 256)
-        weave(0, 1, 256, 512)
+        weave(0, 1, 0, P2)
         for i in range(4, 7):
             pick(i, 1, (other_slot(7, 1), "late", "tab2_w1")[i - 4])
             round_x(i, 1)

from contextlib import ExitStack

import concourse.mybir as mybir

K, H, T, S, T3, S2, P2 = 1024, 1024, 4096, 1024, 2048, 512, 512
FLOPS = 2 * 2 * K * H * S + 2 * 2 * H * S2 * P2

F32 = mybir.dt.float32
BF16 = mybir.dt.bfloat16
I32 = mybir.dt.int32
U32 = mybir.dt.uint32
U16 = mybir.dt.uint16
U8 = mybir.dt.uint8
FP8X4 = mybir.dt.float8_e4m3fn_x4
FP4X4 = mybir.dt.float4_e2m1fn_x4
ALU = mybir.AluOpType
IDENT = mybir.ActivationFunctionType.Identity

P = 128
PACK = 4
PASS = P * PACK
BANK = 512


def tile_list_runway_look_order_kernel(
    tc, tab_words, tab_scales, tab2_words, tab2_scales, w1, w4_words, w4_scales,
    gain, opening, cue, offs, offs2, pos1, pos2, out,
):
    nc = tc.nc
    with ExitStack() as ctx:
        keep = ctx.enter_context(tc.tile_pool(name="keep", bufs=1))
        ring = ctx.enter_context(tc.tile_pool(name="ring", bufs=4))
        psum = ctx.enter_context(tc.psum_pool(name="psum", bufs=1))

        def held(shape, dtype, name):
            return keep.tile(shape, dtype, name=name, align_bytes=64)

        offs_t = held([P, S // 16], U16, "offs_t")
        offs2_t = held([P, S2 // 16], U16, "offs2_t")
        pos_t = [held([P, P2 // 16], U16, "pos%d_t" % i) for i in range(2)]
        tab_w = [held([P, T], I32, "tab_w%d" % a) for a in range(2)]
        tab_s = held([P, T], U8, "tab_s")
        v_rows = held([P, S], U8, "v_rows")
        tab2_w = [held([P, T3], I32, "tab2_w%d" % a) for a in range(2)]
        tab2_s = held([P, T3], U8, "tab2_s")
        w4_raw = [held([P, 2, H], U8, "w4_raw%d" % b) for b in range(2)]
        w4_sraw = held([P, 2, H], U8, "w4_sraw")
        w4_w = [held([P, 2, H], U8, "w4_w%d" % b) for b in range(2)]
        w4_s = [held([P, 2, PASS], U8, "w4_s%d" % b) for b in range(2)]
        w1_raw = {(a, b): held([P, PACK, PASS], F32, "w1_raw%d%d" % (a, b)) for a, b in ((0, 0), (0, 1), (1, 1))}
        w1_last = [held([P, PACK, PASS // 2], F32, "w1_last%d" % half) for half in range(2)]
        w1_w = {(a, b): held([P, PASS], U32, "w1_w%d%d" % (a, b)) for a, b in ((0, 1), (1, 0), (1, 1))}
        w1_s = {(a, b): held([P, PASS], U8, "w1_s%d%d" % (a, b)) for a in range(2) for b in range(2)}
        v_w = [held([P, S], U32, "v_w%d" % a) for a in range(2)]
        v_s = [held([P, S], U8, "v_s%d" % a) for a in range(2)]
        v2_w = {0: held([P, S2], U32, "v2_w0")}
        v2_s = held([P, S2], U8, "v2_s")
        gain_t = held([P, 2, PACK], F32, "gain_t")
        open_t = held([P, 2, PACK], F32, "open_t")
        cue_t = held([P, 4, P2], F32, "cue_t")
        x_w = {(i, b): held([P, P2], U32, "x_w%d%d" % (i, b)) for i in range(2) for b in range(2)}
        x_s = {(i, b): held([P, P2], U8, "x_s%d%d" % (i, b)) for i in range(2) for b in range(2)}

        def bank(n):
            return psum.tile([P, BANK], F32, name="bank%d" % n)

        nc.vector.memset(w4_sraw[:].rearrange("p a t -> p (a t)").bitcast(I32), 0)
        nc.vector.memset(tab_s[:].bitcast(I32), 0)
        for a in range(2):
            nc.vector.memset(v_s[a][:].bitcast(I32), 0)
        nc.vector.memset(tab2_s[:].bitcast(I32), 0)

        def load_planes(tile, scales):
            for r in range(4):
                nc.sync.dma_start(
                    tile[r:P:32, :, :].bitcast(I32),
                    scales[:, r:16:4, :].rearrange("a q t -> q a t").bitcast(I32),
                )

        def load_w1(a, b):
            rows = w1[PASS * a : PASS * (a + 1), PASS * b : PASS * (b + 1)]
            nc.sync.dma_start(w1_raw[a, b][:], rows.rearrange("(p j) c -> p j c", j=PACK))

        def load_w4_words(b):
            part = w4_words[:, :, H * b : H * (b + 1)]
            nc.sync.dma_start(w4_raw[b][:].bitcast(I32), part.rearrange("a p c -> p a c").bitcast(I32))

        def load_words(tile, words):
            nc.sync.dma_start(tile[:], words.rearrange("p n t -> p (n t)").bitcast(I32))

        nc.sync.dma_start(offs_t[:], offs)
        load_w4_words(0)
        load_planes(w4_sraw, w4_scales)
        nc.sync.dma_start(tab_s[0:P:4, :].bitcast(I32), tab_scales.rearrange("a q t -> (a q) t").bitcast(I32))
        load_w1(0, 0)
        load_words(tab_w[0], tab_words[0])
        load_words(tab_w[1], tab_words[1])
        for half in range(2):
            rows = w1[PASS:K, 256 * half : 256 * (half + 1)]
            nc.sync.dma_start(w1_last[half][:], rows.rearrange("(p j) c -> p j c", j=PACK))
        load_w4_words(1)
        nc.sync.dma_start(pos_t[0][:], pos1)
        nc.sync.dma_start(pos_t[1][:], pos2)
        nc.sync.dma_start(gain_t[:], gain.rearrange("(b p t) -> p b t", b=2, t=PACK))
        load_w1(0, 1)
        load_w1(1, 1)
        nc.sync.dma_start(open_t[:], opening.rearrange("(b p t) -> p b t", b=2, t=PACK))
        nc.sync.dma_start(offs2_t[:], offs2)
        for q in range(4):
            nc.sync.dma_start(
                tab2_s[32 * q : 32 * q + 8, :].bitcast(I32),
                tab2_scales[:, 4 * q : 4 * q + 4, :].bitcast(I32),
            )
        load_words(tab2_w[0], tab2_words[0])
        load_words(tab2_w[1], tab2_words[1])
        nc.sync.dma_start(cue_t[:], cue.rearrange("(m p) n -> p m n", p=P))

        w1_bf = {}

        def round_w1(a, b, half):
            if half == 0:
                w1_bf[a, b] = ring.tile([P, PACK, P, PACK], BF16, name="w1_bf", bufs=2, align_bytes=64)
            ms = slice(64 * half, 64 * (half + 1))
            nc.scalar.activation(
                w1_bf[a, b][:, :, ms, :].rearrange("p t m j -> p m t j"),
                w1_raw[a, b][:].rearrange("p j (m t) -> p m t j", t=PACK)[:, ms, :, :],
                IDENT,
            )

        def quantise_w1(a, b):
            nc.vector.quantize_mx(
                out=w1_w[a, b][:].bitcast(FP8X4), scales=w1_s[a, b][:],
                in_=w1_bf[a, b][:].rearrange("p t m j -> p (t m j)"),
            )

        def deal_w4_words(b):
            nc.vector.tensor_copy(
                w4_w[b][:].bitcast(U16).rearrange("p a (t g i) -> p a g t i", t=PACK, i=8),
                w4_raw[b][:].bitcast(U16).rearrange("p a (g i t) -> p a g t i", t=PACK, i=8),
            )

        def deal_w4_scales(b):
            nc.vector.tensor_copy(
                w4_s[b][:].rearrange("p a (t g i) -> p a g t i", t=PACK, i=16),
                w4_sraw[:, :, PASS * b : PASS * (b + 1)].rearrange("p a (g i t) -> p a g t i", t=PACK, i=16),
            )

        def gather_v_words(a, lo, hi):
            nc.vector.tensor_copy(v_w[a][:, lo:hi], tab_w[a][:].bitcast(U32).indirect(offs_t[:, lo // 16 : hi // 16]))

        banks = {}

        def first_pass(i, a, half, kinds=("other", "own")):
            b, t = divmod(i, PACK)
            if a == 0:
                banks[i, half, "own"] = bank(4 * (i % 2) + 2 * half)
                banks[i, half, "other"] = bank(4 * (i % 2) + 2 * half + 1)
            cols = slice(BANK * half, BANK * (half + 1))
            if "other" in kinds:
                nc.tensor.matmul_mx(
                    banks[i, half, "other"][:], lhsT=w4_w[b][:, a, 2 * P * t : 2 * P * (t + 1)].bitcast(FP4X4),
                    lhsT_scale=w4_s[b][:, a, P * t : P * (t + 1)], rhs=v_w[a][:, cols].bitcast(FP8X4),
                    rhs_scale=v_s[a][:, cols], start=(a == 0), stop=(a == 1),
                )
            if "own" in kinds:
                nc.tensor.matmul_mx(
                    banks[i, half, "own"][:], lhsT=w1_w[a, b][:, P * t : P * (t + 1)].bitcast(FP8X4),
                    lhsT_scale=w1_s[a, b][:, P * t : P * (t + 1)], rhs=v_w[a][:, cols].bitcast(FP8X4),
                    rhs_scale=v_s[a][:, cols], start=(a == 0), stop=(a == 1),
                )

        def multiply(i):
            for half in range(2):
                for a in range(2):
                    first_pass(i, a, half)

        others = {}
        top = {}

        def other_slot(i, half):
            return "front%d" % (i % 3) if half == 0 else "back%d" % (i % 2)

        def fetch_other(i):
            if i == 0:
                others["first"] = keep.tile([P, 2 * S], F32, name="w1_last0", align_bytes=64)
            for half in range(2):
                if i < 2:
                    others[i, half] = others["first"][:, S * i + BANK * half : S * i + BANK * (half + 1)]
                else:
                    others[i, half] = keep.tile([P, BANK], F32, name=other_slot(i, half), align_bytes=64)[:]
                nc.scalar.copy(others[i, half], banks[i, half, "other"][:])

        def take_max(i):
            top[i] = ring.tile([P, S], F32, name="top", bufs=4, align_bytes=64)
            for half in range(2):
                nc.vector.tensor_tensor(
                    top[i][:, BANK * half : BANK * (half + 1)], banks[i, half, "own"][:], others[i, half], ALU.max
                )

        picked = {}

        def pick(i, lst, slot=None, parts=1):
            if slot is None:
                picked[i, lst] = ring.tile([P, P2], F32, name="picked", bufs=5, align_bytes=64)
            else:
                picked[i, lst] = keep.tile([P, P2], F32, name=slot, align_bytes=64)
            width = P2 // parts
            for lo in range(0, P2, width):
                offsets = pos_t[lst][:, lo // 16 : (lo + width) // 16]
                nc.vector.tensor_copy(picked[i, lst][:, lo : lo + width], top[i][:].indirect(offsets))

        rows_bf = {}
        woven = {}

        def round_x(i, lst, lo=0, hi=P2):
            b, t = divmod(i, PACK)
            if t == 0:
                rows_bf[lst, b] = ring.tile([P, 2, P2, 2], BF16, name="rows_bf", bufs=4, align_bytes=64)
            bias = open_t[:, b, t : t + 1] if lst == 0 else 0.0
            scale = gain_t[:, b, t : t + 1]
            nc.scalar.activation(rows_bf[lst, b][:, t // 2, lo:hi, t % 2], picked[i, lst][:, lo:hi], IDENT, bias=bias, scale=scale)

        def weave(lst, b, lo, hi):
            if lo == 0:
                woven[lst, b] = keep.tile([P, P2, PACK], BF16, name="woven%d" % lst, align_bytes=64)
            nc.scalar.copy(
                woven[lst, b][:, lo:hi, :].bitcast(U32),
                rows_bf[lst, b][:, :, lo:hi, :].bitcast(U32).rearrange("p u n one -> p n (u one)"),
            )

        def quantise_x(lst, b, lo, hi):
            nc.vector.quantize_mx(
                out=x_w[lst, b][:, lo:hi].bitcast(FP8X4), scales=x_s[lst, b][:, lo:hi],
                in_=woven[lst, b][:, lo:hi, :].rearrange("p n t -> p (n t)"),
            )

        def second_pass(dst, lst, b, m, lo, hi, start, stop):
            nc.tensor.matmul_mx(
                dst, lhsT=v2_w[b][:, P * m : P * (m + 1)].bitcast(FP8X4),
                lhsT_scale=v2_s[4 * b : P, P * m : P * (m + 1)], rhs=x_w[lst, b][:, lo:hi].bitcast(FP8X4),
                rhs_scale=x_s[lst, b][:, lo:hi], start=start, stop=stop,
            )

        nc.vector.tensor_copy(v_rows[:], tab_s[:].indirect(offs_t[:]))
        deal_w4_words(0)
        deal_w4_scales(0)
        deal_w4_scales(1)
        round_w1(0, 0, 0)
        round_w1(0, 0, 1)
        for a in range(2):
            for r in range(4):
                nc.scalar.dma_start(
                    v_s[a][r:P:32, :].bitcast(I32), v_rows[64 * a + 4 * r : 64 * (a + 1) : 16, :].bitcast(I32)
                )
        gather_v_words(0, 0, S)
        w1_w[0, 0] = held([P, PASS], U32, "tab_w0")
        quantise_w1(0, 0)
        for i in range(2):
            for half in range(2):
                first_pass(i, 0, half)
        for half in range(2):
            gather_v_words(1, BANK * half, BANK * (half + 1))
            first_pass(0, 1, half, ("other",))
        for half in range(2):
            first_pass(1, 1, half, ("other",))
        last_bf = [held([P, 2, P, PACK], BF16, "last_bf%d" % pair) for pair in range(2)]
        last_out = [last_bf[pair][:].rearrange("p t m j -> p m t j") for pair in range(2)]
        last_in = [w1_last[half][:].rearrange("p j (m t) -> p m t j", t=PACK) for half in range(2)]

        def quantise_last(pair):
            cols = slice(256 * pair, 256 * (pair + 1))
            nc.vector.quantize_mx(
                out=w1_w[1, 0][:, cols].bitcast(FP8X4), scales=w1_s[1, 0][:, cols],
                in_=last_bf[pair][:].rearrange("p t m j -> p (t m j)"),
            )

        for pair in range(2):
            nc.scalar.activation(last_out[pair][:, 0:64, :, :], last_in[0][:, :, 2 * pair : 2 * pair + 2, :], IDENT)
        nc.vector.tensor_copy(last_out[0][:, 64:P, :, :], last_in[1][:, :, 0:2, :])
        quantise_last(0)
        for i in range(2):
            for half in range(2):
                first_pass(i, 1, half, ("own",))
        fetch_other(0)
        fetch_other(1)
        nc.scalar.activation(last_out[1][:, 64:P, :, :], last_in[1][:, :, 2:4, :], IDENT)
        deal_w4_words(1)

        for i in range(4):
            take_max(i)
            if i == 0:
                quantise_last(1)
            if i == 2:
                quantise_w1(0, 1)
                quantise_w1(1, 1)
            multiply(i + 2)
            if i > 0:
                pick(i - 1, 1, "w1_last0" if i == 1 else other_slot(i, 0))
            pick(i, 0)
            if i < 2:
                round_w1(i, 1, 0)
                round_w1(i, 1, 1)
            fetch_other(i + 2)
            if i == 2:
                for j in range(2):
                    round_x(j, 0)
                    round_x(j, 1)
            if i == 3:
                round_x(2, 0)
                round_x(2, 1)
                round_x(3, 0)

        e1 = []
        e2 = {}
        for i in range(4, 8):
            take_max(i)
            if i < 6:
                multiply(i + 2)
                fetch_other(i + 2)
            if i == 4:
                pick(3, 1, other_slot(4, 0))
                round_x(3, 1)
                weave(0, 0, 0, P2)
            if i == 5:
                nc.vector.tensor_copy(v2_s[:], tab2_s[:].indirect(offs2_t[:]))
                quantise_x(0, 0, 0, P2)
                weave(1, 0, 0, P2)
            if i == 6:
                nc.vector.tensor_copy(v2_w[0][:], tab2_w[0][:].bitcast(U32).indirect(offs2_t[:]))
                quantise_x(1, 0, 0, P2)
                for m in range(4):
                    e1.append(bank(m))
                    second_pass(e1[m][:], 0, 0, m, 0, P2, True, False)
            if i == 7:
                v2_w[1] = held([P, S2], U32, other_slot(7, 0))
                nc.vector.tensor_copy(v2_w[1][:], tab2_w[1][:].bitcast(U32).indirect(offs2_t[:]))
                for half in range(2):
                    for pair in range(2):
                        e2[half, pair] = bank(4 + 2 * half + pair)
                        for mm in range(2):
                            second_pass(e2[half, pair][:, 256 * mm : 256 * (mm + 1)], 1, 0, 2 * pair + mm,
                                        256 * half, 256 * (half + 1), mm == 0, False)
            pick(i, 0, "late" if i == 7 else None)
            round_x(i, 0)
        weave(0, 1, 0, P2)
        for i in range(4, 7):
            pick(i, 1, (other_slot(7, 1), "late", "tab2_w1")[i - 4])
            round_x(i, 1)
        quantise_x(0, 1, 0, P2)
        for m in range(4):
            second_pass(e1[m][:], 0, 1, m, 0, P2, False, True)
        pick(7, 1, "woven0", parts=2)
        for lo in (0, 256):
            round_x(7, 1, lo, lo + 256)
            weave(1, 1, lo, lo + 256)
        for m in range(4):
            nc.vector.tensor_tensor(cue_t[:, m, :], e1[m][:], cue_t[:, m, :], ALU.mult)
        for half in range(2):
            quantise_x(1, 1, 256 * half, 256 * (half + 1))
            for pair in range(2):
                for mm in range(2):
                    second_pass(e2[half, pair][:, 256 * mm : 256 * (mm + 1)], 1, 1, 2 * pair + mm,
                                256 * half, 256 * (half + 1), False, mm == 1)
        out_v = out.rearrange("(m p) n -> p m n", p=P)
        for half in range(2):
            for pair in range(2):
                part = cue_t[:, 2 * pair : 2 * pair + 2, 256 * half : 256 * (half + 1)]
                nc.vector.tensor_tensor(part, e2[half, pair][:].rearrange("p (m n) -> p m n", m=2), part, ALU.mult)
                nc.sync.dma_start(out_v[:, 2 * pair : 2 * pair + 2, 256 * half : 256 * (half + 1)], part)
